import numpy as np
import ml_dtypes


def mxq(x, axis, fmt="e4m3"):
    dtype, down = {"e4m3": (ml_dtypes.float8_e4m3fn, 7), "e5m2": (ml_dtypes.float8_e5m2, 14)}[fmt]
    v = np.moveaxis(np.asarray(x, np.float32).astype(ml_dtypes.bfloat16).astype(np.float64), axis, -1)
    blocks = v.reshape(v.shape[:-1] + (-1, 32))
    amax = np.abs(blocks).max(-1, keepdims=True)
    byte = np.maximum(np.where(amax > 0, np.frexp(amax)[1] - 1 + 127, 0) - down, 1)
    scale = np.exp2(byte - 127.0)
    codes = (blocks / scale).astype(np.float32).astype(dtype).astype(np.float64)
    return np.moveaxis((codes * scale).reshape(v.shape), -1, axis)


WIDE = False


def mx_kscale(k):
    if not WIDE:
        return np.ones(k)
    levels = np.array([10, -10, 5, -5, 0])
    if k % 512:
        return np.exp2(np.random.permutation(np.resize(levels, k // 32))).repeat(32)
    a = np.empty((k // 512, 16))
    for p in range(k // 512):
        a[p, :8] = np.random.permutation(np.resize(levels, 8))
        for g in range(8):
            far = levels[np.abs(levels - a[p, g]) >= 10]
            a[p, g + 8] = far[np.random.randint(len(far))]
    return np.exp2(a.ravel()).repeat(32)


def f64(x):
    return np.asarray(x).astype(np.float64)


def striped(idx):
    return np.tile(idx.reshape(-1, 16).T, (8, 1)).astype(np.uint16)


def unstriped(offs):
    return offs[:16].T.reshape(-1).astype(np.int64)


E2M1 = np.array([0.0, 0.5, 1.0, 1.5, 2.0, 3.0, 4.0, 6.0, -0.0, -0.5, -1.0, -1.5, -2.0, -3.0, -4.0, -6.0])


def pack_weight(w, fmt):
    k, n = w.shape
    w = f64(np.asarray(w, np.float32).astype(ml_dtypes.bfloat16)).reshape(k // 32, 32, n)
    amax = np.abs(w).max(1)
    if fmt == "e4m3":
        byte = np.frexp(amax)[1] - 1 + 127 - 7
    else:
        mant, ex = np.frexp(amax / 6.0)
        byte = np.where(mant > 0.5, ex, ex - 1) + 127
    byte = np.clip(np.where(amax > 0, byte, 1), 1, 254)
    scaled = (w * np.exp2(127.0 - byte)[:, None, :]).reshape(k, n).astype(np.float32)
    by_word = np.ascontiguousarray(scaled.reshape(k // 512, 128, 4, n).transpose(0, 1, 3, 2))
    if fmt == "e4m3":
        words = by_word.astype(ml_dtypes.float8_e4m3fn).view(np.uint8)
    else:
        c = by_word.astype(ml_dtypes.float4_e2m1fn).view(np.uint8) & 0xF
        words = (c[..., 0::2] | (c[..., 1::2] << 4)).reshape(k // 512, 128, 2 * n)
    return np.ascontiguousarray(words), np.ascontiguousarray(byte.astype(np.uint8).reshape(k // 512, 16, n))


def unpack_weight(words, scales, fmt):
    g, _, n = scales.shape
    words = np.ascontiguousarray(words).reshape(g, 128, n, -1)
    if fmt == "e4m3":
        vals = words.view(ml_dtypes.float8_e4m3fn).astype(np.float64)
    else:
        nib = np.empty((g, 128, n, 4), np.uint8)
        nib[..., 0::2] = words & 0xF
        nib[..., 1::2] = words >> 4
        vals = E2M1[nib]
    vals = vals * np.repeat(np.exp2(scales.astype(np.float64) - 127.0), 8, axis=1)[..., None]
    return vals.transpose(0, 1, 3, 2).reshape(g * 512, n)


def gelu(v):
    return 0.5 * v * (1.0 + np.tanh(np.sqrt(2.0 / np.pi) * (v + 0.044715 * v**3)))


def striped8(idx):
    return np.concatenate([v.reshape(-1, 16).T for v in idx]).astype(np.uint16)


def unstriped8(offs):
    return np.stack([offs[16 * g:16 * g + 16].T.reshape(-1) for g in range(8)]).astype(np.int64)


def heads(h, wgt, idx8):
    r = np.arange(h.shape[0])
    return wgt[r // 4 % 128] * h[r[:, None], idx8[r % 512 // 64]]


def put_heads(h, wgs, idx8, t2):
    r = np.arange(h.shape[0])
    page = np.zeros((h.shape[0], t2))
    page[r[:, None], idx8[r % 512 // 64]] = wgs[r // 4 % 128] * h
    return page


K, H, N, T, S, P, T2 = 1024, 1024, 512, 4096, 1024, 512, 1024

def setup_inputs():
    n = np.random.standard_normal
    s = mx_kscale(K)[:, None]
    u = mx_kscale(H)[:, None]
    d = {}
    d["tab_words"], d["tab_scales"] = pack_weight(n((K, T)) * s, "e4m3")
    d["offs"] = striped(np.random.permutation(T)[:S])
    d["w1_words"], d["w1_scales"] = pack_weight(n((K, H)) / K**0.5 / s * u.T, "e2m1")
    d["sound"] = (n((K, S)) * s).astype(np.float32)
    d["w2"] = (n((K, H)) / K**0.5 / s * u.T).astype(np.float32)
    d["offs2"] = striped8(np.stack([np.random.permutation(S)[:P] for _ in range(8)]))
    d["wgt"] = np.repeat(np.random.uniform(0.5, 2.0, (8, P)), 16, axis=0).astype(np.float32)
    d["gain"] = np.exp(0.3 * n(H)).astype(np.float32)
    d["w3_words"], d["w3_scales"] = pack_weight(1.5 * n((H, N)) / H**0.5 / u, "e4m3")
    d["base"] = (0.5 * n(N)).astype(np.float32)
    d["offs3"] = striped8(np.stack([np.random.permutation(T2)[:P] for _ in range(8)]))
    d["wgo"] = np.repeat(np.random.uniform(0.5, 2.0, (8, P)), 16, axis=0).astype(np.float32)
    return d

def reference(tab_words, tab_scales, offs, w1_words, w1_scales, sound, w2, offs2, wgt, gain,
              w3_words, w3_scales, base, offs3, wgo):
    v = unpack_weight(tab_words, tab_scales, "e4m3")[:, unstriped(offs)]
    w1 = unpack_weight(w1_words, w1_scales, "e2m1")
    a = w1.T @ v
    b = mxq(f64(w2), 0, "e4m3").T @ mxq(f64(sound), 0, "e4m3")
    h = np.maximum(a, b)
    x = heads(h, f64(wgt), unstriped8(offs2)) * f64(gain)[:, None]
    w3 = unpack_weight(w3_words, w3_scales, "e4m3")
    y = w3.T @ mxq(x, 0, "e4m3")
    need = np.log(np.abs(y) + 1.0) + f64(base)[:, None]
    return put_heads(need, f64(wgo), unstriped8(offs3), T2)

@@ -1,0 +1,299 @@
+from contextlib import ExitStack
+
+import concourse.mybir as mybir
+
+K, H, N, T, S, M, T2 = 1024, 1024, 512, 4096, 1024, 512, 1024
+FLOPS = 2 * (2 * K * H * S + H * N * M)
+
+F32 = mybir.dt.float32
+BF16 = mybir.dt.bfloat16
+I32 = mybir.dt.int32
+U32 = mybir.dt.uint32
+U16 = mybir.dt.uint16
+U8 = mybir.dt.uint8
+FP8X4 = mybir.dt.float8_e4m3fn_x4
+FP4X4 = mybir.dt.float4_e2m1fn_x4
+ACT = mybir.ActivationFunctionType
+ALU = mybir.AluOpType
+
+P = 128
+PACK = 4
+PASS = P * PACK
+HALF = 512
+MH = M // 2
+
+
+def tile_list_hoof_trim_slots_kernel(
+    tc, tab_words, tab_scales, offs, w1_words, w1_scales, sound, w2, offs2, wgt, gain,
+    w3_words, w3_scales, base, offs3, wgo, out,
+):
+    nc = tc.nc
+    with ExitStack() as ctx:
+        lists = ctx.enter_context(tc.tile_pool(name="lists", bufs=1))
+        keep = ctx.enter_context(tc.tile_pool(name="keep", bufs=1))
+        ring = ctx.enter_context(tc.tile_pool(name="ring", bufs=1))
+        psum = ctx.enter_context(tc.psum_pool(name="psum", bufs=4))
+
+        idx = lists.tile([P, S // 16], U16, name="idx")
+        idx2 = lists.tile([P, M // 16], U16, name="idx2")
+        idx3 = lists.tile([P, M // 16], U16, name="idx3")
+
+        def kept(shape, dtype, name):
+            return keep.tile(shape, dtype, name=name, align_bytes=64)
+
+        def raw_tile(width, name):
+            return ring.tile([P, PACK, width], F32, name=name, tag="raw", bufs=6, align_bytes=64)
+
+        def stage_tile(width, name):
+            return ring.tile([P, PACK * width], BF16, name=name, tag="stage", bufs=4, align_bytes=64)
+
+        def load_scale_rows(queue, plane, scales):
+            for q in range(4):
+                queue.dma_start(
+                    out=plane[32 * q : 32 * q + 4, :, :].bitcast(I32),
+                    in_=scales[:, 4 * q : 4 * q + 4, :].rearrange("a r c -> r a c").bitcast(I32),
+                )
+
+        def load_packed_scale_rows(queue, plane, scales):
+            for q in range(4):
+                queue.dma_start(
+                    out=plane[32 * q : 32 * q + 8, :].bitcast(I32),
+                    in_=scales[:, 4 * q : 4 * q + 4, :].bitcast(I32),
+                )
+
+        def load_rows(src, a, cols, name):
+            raw = raw_tile(HALF, name)
+            nc.sync.dma_start(
+                out=raw[:],
+                in_=src[a * PASS : (a + 1) * PASS, cols * HALF : (cols + 1) * HALF].rearrange("(p j) c -> p j c", j=PACK),
+            )
+            return raw
+
+        def copy_on(engine, out_ap, in_ap):
+            if engine == "scalar":
+                nc.scalar.copy(out=out_ap, in_=in_ap)
+            else:
+                nc.vector.tensor_copy(out=out_ap, in_=in_ap)
+
+        def round_plain(engine, raw, width, name):
+            st = stage_tile(width, name)
+            copy_on(
+                engine,
+                st[:].rearrange("p (c i j) -> p c j i", i=4, j=PACK),
+                raw[:].rearrange("p j (c i) -> p c j i", i=4),
+            )
+            return st
+
+        def round_dealt(engine, raw, name):
+            st = stage_tile(HALF, name)
+            copy_on(
+                engine,
+                st[:].rearrange("p (t m j) -> p m j t", t=PACK, j=PACK),
+                raw[:].rearrange("p j (m t) -> p m j t", t=PACK),
+            )
+            return st
+
+        def quantise(st, width, name):
+            codes = kept([P, width], U32, name + "_codes")
+            scales = kept([P, width], U8, name + "_scales")
+            nc.vector.quantize_mx(out=codes[:].bitcast(FP8X4), scales=scales[:], in_=st[:])
+            return codes, scales
+
+        tab_sc = kept([P, 2, T], U8, "tab_sc")
+        w1_sc_raw = kept([P, 2, H], U8, "w1_sc_raw")
+        w3_sc_raw = kept([P, N], U8, "w3_sc_raw")
+        v_sc = {a: kept([P, S], U8, f"v_sc{a}") for a in range(2)}
+        for plane in (tab_sc, w1_sc_raw, w3_sc_raw):
+            nc.vector.memset(plane[:].bitcast(I32), 0)
+        pages = [kept([P, T2], F32, f"page{i}") for i in range(PACK)]
+        for page in pages:
+            nc.vector.memset(page[:], 0.0)
+
+        w2_raw = {}
+        sound_raw = {}
+        tab = {}
+        nc.sync.dma_start(idx[:], offs)
+        for a in range(2):
+            w2_raw[0, a] = load_rows(w2, a, 0, f"w2_raw0{a}")
+        w1_raw = kept([P, 2, 2 * H], U8, "w1_raw")
+        nc.sync.dma_start(out=w1_raw[:].bitcast(I32), in_=w1_words.rearrange("a p c -> p a c").bitcast(I32))
+        gain_sb = kept([P, 2, PACK], F32, "gain_sb")
+        nc.sync.dma_start(out=gain_sb[:], in_=gain.rearrange("(b p i) -> p b i", b=2, i=PACK))
+        wgt_sb = kept([P, M], F32, "wgt_sb")
+        nc.sync.dma_start(out=wgt_sb[:], in_=wgt)
+        nc.sync.dma_start(idx2[:], offs2)
+        nc.sync.dma_start(idx3[:], offs3)
+        load_scale_rows(nc.sync, tab_sc, tab_scales)
+        for a in range(2):
+            sound_raw[0, a] = load_rows(sound, a, 0, f"sound_raw0{a}")
+        load_scale_rows(nc.sync, w1_sc_raw, w1_scales)
+        for a in range(2):
+            tab[a] = kept([P, T], I32, f"tab{a}")
+            nc.sync.dma_start(out=tab[a][:], in_=tab_words[a].rearrange("p t i -> p (t i)").bitcast(I32))
+        for a in range(2):
+            sound_raw[1, a] = load_rows(sound, a, 1, f"sound_raw1{a}")
+        for a in range(2):
+            w2_raw[1, a] = load_rows(w2, a, 1, f"w2_raw1{a}")
+        w3_raw = kept([P, 2, N], I32, "w3_raw")
+        nc.sync.dma_start(out=w3_raw[:], in_=w3_words.rearrange("a p c i -> p a (c i)").bitcast(I32))
+        load_packed_scale_rows(nc.sync, w3_sc_raw, w3_scales)
+        base_sb = kept([P, PACK], F32, "base_sb")
+        nc.sync.dma_start(out=base_sb[:], in_=base.rearrange("(p i) -> p i", i=PACK))
+        wgo_sb = kept([P, M], F32, "wgo_sb")
+        nc.sync.dma_start(out=wgo_sb[:], in_=wgo)
+
+        w2q = {}
+        soundq = {}
+        for a in range(2):
+            w2q[0, a] = quantise(round_dealt("scalar", w2_raw[0, a], f"w2_st0{a}"), HALF, f"w2q0{a}")
+
+        w1c = kept([P, 2, H], U16, "w1c")
+        w1s = kept([P, 2, H], U8, "w1s")
+        nc.vector.tensor_copy(
+            out=w1c[:].rearrange("p a (b t m) -> p (a b) t m", b=2, t=PACK),
+            in_=w1_raw[:].bitcast(U16).rearrange("p a (b m t) -> p (a b) t m", b=2, t=PACK),
+        )
+
+        for a in range(2):
+            nc.vector.tensor_copy(out=v_sc[a][:], in_=tab_sc[:, a, :].indirect(idx[:]))
+        for a in range(2):
+            soundq[0, a] = quantise(round_plain("scalar", sound_raw[0, a], HALF, f"sound_st0{a}"), HALF, f"soundq0{a}")
+
+
+        h = {(b, i): kept([P, S], F32, f"h{b}{i}") for b in range(2) for i in range(PACK)}
+        v_c = {}
+
+        def product_given(b, i, c, tag):
+            acc = psum.tile([P, HALF], F32, name=f"given{b}{i}{c}", tag=tag)
+            cols = slice(P * i, P * (i + 1))
+            for a in range(2):
+                nc.tensor.matmul_mx(
+                    out=acc[:],
+                    lhsT=w2q[b, a][0][:, cols].bitcast(FP8X4), lhsT_scale=w2q[b, a][1][:, cols],
+                    rhs=soundq[c, a][0][:].bitcast(FP8X4), rhs_scale=soundq[c, a][1][:],
+                    start=(a == 0), stop=(a == 1),
+                )
+            return acc
+
+        def product_picked(b, i, c, tag):
+            acc = psum.tile([P, HALF], F32, name=f"picked{b}{i}{c}", tag=tag)
+            c0 = HALF * b + P * i
+            for a in range(2):
+                nc.tensor.matmul_mx(
+                    out=acc[:],
+                    lhsT=w1c[:, a, c0 : c0 + P].bitcast(FP4X4), lhsT_scale=w1s[:, a, c0 : c0 + P],
+                    rhs=v_c[c, a][:].bitcast(FP8X4), rhs_scale=v_sc[a][:, c * HALF : (c + 1) * HALF],
+                    start=(a == 0), stop=(a == 1),
+                )
+            return acc
+
+        def h_cols(b, i, c):
+            return h[b, i][:, c * HALF : (c + 1) * HALF]
+
+        def park(product, b, i, c):
+            nc.scalar.copy(out=h_cols(b, i, c), in_=product(b, i, c, "early")[:])
+
+        def meet(product, b, i, c):
+            nc.vector.tensor_tensor(out=h_cols(b, i, c), in0=product(b, i, c, "late")[:], in1=h_cols(b, i, c), op=ALU.max)
+
+        def pick_words(a, c):
+            v_c[c, a] = kept([P, HALF], U32, f"v_c{c}{a}")
+            nc.vector.tensor_copy(
+                out=v_c[c, a][:], in_=tab[a][:].bitcast(U32).indirect(idx[:, c * HALF // 16 : (c + 1) * HALF // 16])
+            )
+
+        for i in range(PACK):
+            park(product_given, 0, i, 0)
+
+        wg = {}
+        for b in range(2):
+            for i in range(PACK):
+                wg[b, i] = kept([P, M], F32, f"wg{b}{i}")
+                nc.scalar.activation(out=wg[b, i][:], in_=wgt_sb[:], func=ACT.Copy, scale=gain_sb[:, b, i : i + 1])
+
+        for c in range(2):
+            pick_words(0, c)
+        nc.vector.tensor_copy(
+            out=w1s[:].rearrange("p a (b t m) -> p (a b) t m", b=2, t=PACK),
+            in_=w1_sc_raw[:].rearrange("p a (b m t) -> p (a b) t m", b=2, t=PACK),
+        )
+        for c in range(2):
+            pick_words(1, c)
+        for i in range(PACK):
+            meet(product_picked, 0, i, 0)
+
+        st0 = round_plain("scalar", sound_raw[1, 0], HALF, "sound_st10")
+        for i in range(PACK):
+            park(product_picked, 0, i, 1)
+        st1 = round_plain("vector", sound_raw[1, 1], HALF, "sound_st11")
+        soundq[1, 0] = quantise(st0, HALF, "soundq10")
+        soundq[1, 1] = quantise(st1, HALF, "soundq11")
+
+        picked0 = raw_tile(M, "picked0")
+        for i in range(PACK):
+            meet(product_given, 0, i, 1)
+            nc.vector.tensor_tensor(out=picked0[:, i, :], in0=h[0, i][:].indirect(idx2[:]), in1=wg[0, i][:], op=ALU.mult)
+
+        for a in range(2):
+            w2q[1, a] = quantise(round_dealt("scalar", w2_raw[1, a], f"w2_st1{a}"), HALF, f"w2q1{a}")
+        for i in range(PACK):
+            for c in range(2):
+                park(product_picked, 1, i, c)
+        xq0 = quantise(round_plain("scalar", picked0, M, "x_st0"), M, "xq0")
+        w3c = kept([P, 2, N], U32, "w3c")
+        nc.scalar.copy(
+            out=w3c[:].rearrange("p a (t m) -> p a t m", t=PACK),
+            in_=w3_raw[:].bitcast(U32).rearrange("p a (m t) -> p a t m", t=PACK),
+        )
+
+        w3s = kept([P, N], U8, "w3s")
+        nc.vector.tensor_copy(
+            out=w3s[:].rearrange("p (t m) -> p t m", t=PACK),
+            in_=w3_sc_raw[:].rearrange("p (m t) -> p t m", t=PACK),
+        )
+
+        picked1 = [raw_tile(MH, f"picked1{u}") for u in range(2)]
+
+        def pick_x(i, u):
+            nc.vector.tensor_tensor(
+                out=picked1[u][:, i, :],
+                in0=h[1, i][:].indirect(idx2[:, u * MH // 16 : (u + 1) * MH // 16]),
+                in1=wg[1, i][:, u * MH : (u + 1) * MH],
+                op=ALU.mult,
+            )
+
+        for i in range(PACK):
+            for c in range(2):
+                meet(product_given, 1, i, c)
+            pick_x(i, 0)
+        x_st = round_plain("scalar", picked1[0], MH, "x_st10")
+        xq1 = {}
+        xq1[0] = quantise(x_st, MH, "xq10")
+        for i in range(PACK):
+            pick_x(i, 1)
+        xq1[1] = quantise(round_plain("scalar", picked1[1], MH, "x_st11"), MH, "xq11")
+
+        out_rows = out.rearrange("(p i) c -> p i c", i=PACK)
+        for u in range(2):
+            ms = slice(u * MH, (u + 1) * MH)
+            for i in range(PACK):
+                cols = slice(P * i, P * (i + 1))
+                y = psum.tile([P, MH], F32, name=f"y{u}{i}", tag="early")
+                nc.tensor.matmul_mx(
+                    out=y[:], lhsT=w3c[:, 0, cols].bitcast(FP8X4), lhsT_scale=w3s[:, cols],
+                    rhs=xq0[0][:, ms].bitcast(FP8X4), rhs_scale=xq0[1][:, ms], start=True, stop=False,
+                )
+                nc.tensor.matmul_mx(
+                    out=y[:], lhsT=w3c[:, 1, cols].bitcast(FP8X4), lhsT_scale=w3s[4:P, cols],
+                    rhs=xq1[u][0][:].bitcast(FP8X4), rhs_scale=xq1[u][1][:], start=False, stop=True,
+                )
+                need = ring.tile([P, MH], F32, name=f"need{u}{i}", tag="need", bufs=4)
+                nc.scalar.activation(out=need[:], in_=y[:], func=ACT.Abs)
+                nc.scalar.activation(out=need[:], in_=need[:], func=ACT.Ln, bias=1.0)
+                nc.scalar.activation(out=need[:], in_=need[:], func=ACT.Identity, bias=base_sb[:, i : i + 1])
+                nc.vector.tensor_tensor(
+                    out=pages[i][:].indirect(idx3[:, u * MH // 16 : (u + 1) * MH // 16]),
+                    in0=need[:], in1=wgo_sb[:, ms], op=ALU.mult,
+                )
+                if u == 1:
+                    nc.sync.dma_start(out=out_rows[:, i, :], in_=pages[i][:])

@@ -42,10 +42,10 @@ def tile_list_hoof_trim_slots_kernel(
             return keep.tile(shape, dtype, name=name, align_bytes=64)
 
         def raw_tile(width, name):
-            return ring.tile([P, PACK, width], F32, name=name, tag="raw", bufs=6, align_bytes=64)
+            return ring.tile([P, PACK, width], F32, name=name, tag="raw", bufs=5, align_bytes=64)
 
         def stage_tile(width, name):
-            return ring.tile([P, PACK * width], BF16, name=name, tag="stage", bufs=4, align_bytes=64)
+            return ring.tile([P, PACK * width], BF16, name=name, tag="stage", bufs=3, align_bytes=64)
 
         def load_scale_rows(queue, plane, scales):
             for q in range(4):
@@ -75,28 +75,34 @@ def tile_list_hoof_trim_slots_kernel(
             else:
                 nc.vector.tensor_copy(out=out_ap, in_=in_ap)
 
-        def round_plain(engine, raw, width, name):
-            st = stage_tile(width, name)
+        def interleave(engine, st, rows):
             copy_on(
                 engine,
-                st[:].rearrange("p (c i j) -> p c j i", i=4, j=PACK),
-                raw[:].rearrange("p j (c i) -> p c j i", i=4),
+                st.rearrange("p (c i j) -> p c j i", i=4, j=PACK),
+                rows.rearrange("p j (c i) -> p c j i", i=4),
             )
-            return st
+
+        def deal(engine, st, raw):
+            copy_on(
+                engine,
+                st.rearrange("p (t m j) -> p m j t", t=PACK, j=PACK),
+                raw[:].rearrange("p j (m t) -> p m j t", t=PACK),
+            )
+
+        def round_plain(engine, raw, width, name):
+            st = stage_tile(width, name)
+            interleave(engine, st[:], raw[:])
+            return st[:]
 
         def round_dealt(engine, raw, name):
             st = stage_tile(HALF, name)
-            copy_on(
-                engine,
-                st[:].rearrange("p (t m j) -> p m j t", t=PACK, j=PACK),
-                raw[:].rearrange("p j (m t) -> p m j t", t=PACK),
-            )
-            return st
+            deal(engine, st[:], raw)
+            return st[:]
 
         def quantise(st, width, name):
             codes = kept([P, width], U32, name + "_codes")
             scales = kept([P, width], U8, name + "_scales")
-            nc.vector.quantize_mx(out=codes[:].bitcast(FP8X4), scales=scales[:], in_=st[:])
+            nc.vector.quantize_mx(out=codes[:].bitcast(FP8X4), scales=scales[:], in_=st)
             return codes, scales
 
         tab_sc = kept([P, 2, T], U8, "tab_sc")
@@ -112,11 +118,18 @@ def tile_list_hoof_trim_slots_kernel(
         w2_raw = {}
         sound_raw = {}
         tab = {}
+        def load_w1_words(b):
+            w1_raw[b] = kept([P, 2, 2 * HALF], U8, f"w1_raw{b}")
+            nc.sync.dma_start(
+                out=w1_raw[b][:].bitcast(I32),
+                in_=w1_words[:, :, 2 * HALF * b : 2 * HALF * (b + 1)].rearrange("a p c -> p a c").bitcast(I32),
+            )
+
+        w1_raw = {}
         nc.sync.dma_start(idx[:], offs)
         for a in range(2):
             w2_raw[0, a] = load_rows(w2, a, 0, f"w2_raw0{a}")
-        w1_raw = kept([P, 2, 2 * H], U8, "w1_raw")
-        nc.sync.dma_start(out=w1_raw[:].bitcast(I32), in_=w1_words.rearrange("a p c -> p a c").bitcast(I32))
+        load_w1_words(0)
         gain_sb = kept([P, 2, PACK], F32, "gain_sb")
         nc.sync.dma_start(out=gain_sb[:], in_=gain.rearrange("(b p i) -> p b i", b=2, i=PACK))
         wgt_sb = kept([P, M], F32, "wgt_sb")
@@ -125,18 +138,19 @@ def tile_list_hoof_trim_slots_kernel(
         nc.sync.dma_start(idx3[:], offs3)
         load_scale_rows(nc.sync, tab_sc, tab_scales)
         for a in range(2):
-            sound_raw[0, a] = load_rows(sound, a, 0, f"sound_raw0{a}")
-        load_scale_rows(nc.sync, w1_sc_raw, w1_scales)
-        for a in range(2):
             tab[a] = kept([P, T], I32, f"tab{a}")
             nc.sync.dma_start(out=tab[a][:], in_=tab_words[a].rearrange("p t i -> p (t i)").bitcast(I32))
-        for a in range(2):
-            sound_raw[1, a] = load_rows(sound, a, 1, f"sound_raw1{a}")
+            if a == 0:
+                load_scale_rows(nc.sync, w1_sc_raw, w1_scales)
+        load_packed_scale_rows(nc.sync, w3_sc_raw, w3_scales)
+        for c in range(2):
+            for a in range(2):
+                sound_raw[c, a] = load_rows(sound, a, c, f"sound_raw{c}{a}")
+        load_w1_words(1)
         for a in range(2):
             w2_raw[1, a] = load_rows(w2, a, 1, f"w2_raw1{a}")
         w3_raw = kept([P, 2, N], I32, "w3_raw")
         nc.sync.dma_start(out=w3_raw[:], in_=w3_words.rearrange("a p c i -> p a (c i)").bitcast(I32))
-        load_packed_scale_rows(nc.sync, w3_sc_raw, w3_scales)
         base_sb = kept([P, PACK], F32, "base_sb")
         nc.sync.dma_start(out=base_sb[:], in_=base.rearrange("(p i) -> p i", i=PACK))
         wgo_sb = kept([P, M], F32, "wgo_sb")
@@ -147,18 +161,20 @@ def tile_list_hoof_trim_slots_kernel(
         for a in range(2):
             w2q[0, a] = quantise(round_dealt("scalar", w2_raw[0, a], f"w2_st0{a}"), HALF, f"w2q0{a}")
 
-        w1c = kept([P, 2, H], U16, "w1c")
+        w1c = {}
         w1s = kept([P, 2, H], U8, "w1s")
-        nc.vector.tensor_copy(
-            out=w1c[:].rearrange("p a (b t m) -> p (a b) t m", b=2, t=PACK),
-            in_=w1_raw[:].bitcast(U16).rearrange("p a (b m t) -> p (a b) t m", b=2, t=PACK),
-        )
 
+        def deal_w1_words(engine, b):
+            w1c[b] = kept([P, 2, HALF], U16, f"w1c{b}")
+            copy_on(
+                engine,
+                w1c[b][:].rearrange("p a (t m) -> p a t m", t=PACK),
+                w1_raw[b][:].bitcast(U16).rearrange("p a (m t) -> p a t m", t=PACK),
+            )
+
+        deal_w1_words("vector", 0)
         for a in range(2):
             nc.vector.tensor_copy(out=v_sc[a][:], in_=tab_sc[:, a, :].indirect(idx[:]))
-        for a in range(2):
-            soundq[0, a] = quantise(round_plain("scalar", sound_raw[0, a], HALF, f"sound_st0{a}"), HALF, f"soundq0{a}")
-
 
         h = {(b, i): kept([P, S], F32, f"h{b}{i}") for b in range(2) for i in range(PACK)}
         v_c = {}
@@ -181,7 +197,7 @@ def tile_list_hoof_trim_slots_kernel(
             for a in range(2):
                 nc.tensor.matmul_mx(
                     out=acc[:],
-                    lhsT=w1c[:, a, c0 : c0 + P].bitcast(FP4X4), lhsT_scale=w1s[:, a, c0 : c0 + P],
+                    lhsT=w1c[b][:, a, P * i : P * (i + 1)].bitcast(FP4X4), lhsT_scale=w1s[:, a, c0 : c0 + P],
                     rhs=v_c[c, a][:].bitcast(FP8X4), rhs_scale=v_sc[a][:, c * HALF : (c + 1) * HALF],
                     start=(a == 0), stop=(a == 1),
                 )
@@ -202,14 +218,20 @@ def tile_list_hoof_trim_slots_kernel(
                 out=v_c[c, a][:], in_=tab[a][:].bitcast(U32).indirect(idx[:, c * HALF // 16 : (c + 1) * HALF // 16])
             )
 
-        for i in range(PACK):
-            park(product_given, 0, i, 0)
-
+        picked11 = kept([P, PACK * MH], F32, "picked11")
         wg = {}
         for b in range(2):
             for i in range(PACK):
-                wg[b, i] = kept([P, M], F32, f"wg{b}{i}")
-                nc.scalar.activation(out=wg[b, i][:], in_=wgt_sb[:], func=ACT.Copy, scale=gain_sb[:, b, i : i + 1])
+                scale = gain_sb[:, b, i : i + 1]
+                if (b, i) == (1, PACK - 1):
+                    wg_last = kept([P, MH], F32, "wg_last")
+                    wg[b, i] = [picked11[:, 0:MH], wg_last[:]]
+                    for u in range(2):
+                        nc.scalar.activation(out=wg[b, i][u], in_=wgt_sb[:, u * MH : (u + 1) * MH], func=ACT.Copy, scale=scale)
+                else:
+                    both = kept([P, M], F32, f"wg{b}{i}")
+                    wg[b, i] = [both[:, 0:MH], both[:, MH:M], both[:]]
+                    nc.scalar.activation(out=both[:], in_=wgt_sb[:], func=ACT.Copy, scale=scale)
 
         for c in range(2):
             pick_words(0, c)
@@ -219,59 +241,73 @@ def tile_list_hoof_trim_slots_kernel(
         )
         for c in range(2):
             pick_words(1, c)
-        for i in range(PACK):
-            meet(product_picked, 0, i, 0)
-
-        st0 = round_plain("scalar", sound_raw[1, 0], HALF, "sound_st10")
-        for i in range(PACK):
-            park(product_picked, 0, i, 1)
-        st1 = round_plain("vector", sound_raw[1, 1], HALF, "sound_st11")
-        soundq[1, 0] = quantise(st0, HALF, "soundq10")
-        soundq[1, 1] = quantise(st1, HALF, "soundq11")
-
-        picked0 = raw_tile(M, "picked0")
-        for i in range(PACK):
-            meet(product_given, 0, i, 1)
-            nc.vector.tensor_tensor(out=picked0[:, i, :], in0=h[0, i][:].indirect(idx2[:]), in1=wg[0, i][:], op=ALU.mult)
+        w3s = kept([P, N], U8, "w3s")
+        nc.vector.tensor_copy(
+            out=w3s[:].rearrange("p (t m) -> p t m", t=PACK),
+            in_=w3_sc_raw[:].rearrange("p (m t) -> p t m", t=PACK),
+        )
+        for c in range(2):
+            for i in range(PACK):
+                park(product_picked, 0, i, c)
 
         for a in range(2):
-            w2q[1, a] = quantise(round_dealt("scalar", w2_raw[1, a], f"w2_st1{a}"), HALF, f"w2q1{a}")
+            soundq[0, a] = quantise(round_plain("vector", sound_raw[0, a], HALF, f"sound_st0{a}"), HALF, f"soundq0{a}")
+        for i in range(PACK):
+            meet(product_given, 0, i, 0)
+        soundq[1, 0] = quantise(round_plain("scalar", sound_raw[1, 0], HALF, "sound_st10"), HALF, "soundq10")
+        last_codes = kept([P, HALF], U32, "soundq11_codes")
+        last_scales = kept([P, HALF], U8, "soundq11_scales")
+        for part, engine in enumerate(("vector", "scalar")):
+            cols = slice(part * MH, (part + 1) * MH)
+            st = stage_tile(MH, f"sound_st11{part}")
+            interleave(engine, st[:], sound_raw[1, 1][:, :, cols])
+            nc.vector.quantize_mx(out=last_codes[:, cols].bitcast(FP8X4), scales=last_scales[:, cols], in_=st[:])
+        soundq[1, 1] = (last_codes, last_scales)
+        deal_w1_words("scalar", 1)
+
+        def pick_x(dst, b, i, first, count):
+            nc.vector.tensor_tensor(
+                out=dst,
+                in0=h[b, i][:].indirect(idx2[:, first // 16 : (first + count) // 16]),
+                in1=wg[b, i][first // MH if count == MH else 2],
+                op=ALU.mult,
+            )
+
+        picked0 = kept([P, 5 * M], F32, "picked0")
+        for i in range(PACK):
+            meet(product_given, 0, i, 1)
+            if i < PACK - 1:
+                pick_x(picked0[:, i * M : (i + 1) * M], 0, i, 0, M)
+        w2q[1, 0] = quantise(round_dealt("scalar", w2_raw[1, 0], "w2_st10"), HALF, "w2q10")
+        st = picked0[:, 3 * M : 5 * M].bitcast(BF16)
+        deal("scalar", st, w2_raw[1, 1])
+        w2q[1, 1] = quantise(st, HALF, "w2q11")
+        pick_x(picked0[:, 3 * M : 4 * M], 0, 3, 0, M)
+
         for i in range(PACK):
             for c in range(2):
                 park(product_picked, 1, i, c)
-        xq0 = quantise(round_plain("scalar", picked0, M, "x_st0"), M, "xq0")
+        st = stage_tile(M, "x_st0")
+        interleave("scalar", st[:], picked0[:, 0 : PACK * M].rearrange("p (j c) -> p j c", j=PACK))
+        xq0 = quantise(st[:], M, "xq0")
         w3c = kept([P, 2, N], U32, "w3c")
         nc.scalar.copy(
             out=w3c[:].rearrange("p a (t m) -> p a t m", t=PACK),
             in_=w3_raw[:].bitcast(U32).rearrange("p a (m t) -> p a t m", t=PACK),
         )
 
-        w3s = kept([P, N], U8, "w3s")
-        nc.vector.tensor_copy(
-            out=w3s[:].rearrange("p (t m) -> p t m", t=PACK),
-            in_=w3_sc_raw[:].rearrange("p (m t) -> p t m", t=PACK),
-        )
-
-        picked1 = [raw_tile(MH, f"picked1{u}") for u in range(2)]
-
-        def pick_x(i, u):
-            nc.vector.tensor_tensor(
-                out=picked1[u][:, i, :],
-                in0=h[1, i][:].indirect(idx2[:, u * MH // 16 : (u + 1) * MH // 16]),
-                in1=wg[1, i][:, u * MH : (u + 1) * MH],
-                op=ALU.mult,
-            )
-
+        picked10 = raw_tile(MH, "picked10")
         for i in range(PACK):
             for c in range(2):
                 meet(product_given, 1, i, c)
-            pick_x(i, 0)
-        x_st = round_plain("scalar", picked1[0], MH, "x_st10")
-        xq1 = {}
-        xq1[0] = quantise(x_st, MH, "xq10")
-        for i in range(PACK):
-            pick_x(i, 1)
-        xq1[1] = quantise(round_plain("scalar", picked1[1], MH, "x_st11"), MH, "xq11")
+            pick_x(picked10[:, i, :], 1, i, 0, MH)
+        for i in range(2):
+            pick_x(picked11[:, i * MH : (i + 1) * MH], 1, i, MH, MH)
+        st = picked11[:, 2 * MH : 4 * MH].bitcast(BF16)
+        interleave("scalar", st, picked10[:])
+        xq1 = {0: quantise(st, MH, "xq10")}
+        for i in range(2, PACK):
+            pick_x(picked11[:, i * MH : (i + 1) * MH], 1, i, MH, MH)
 
         out_rows = out.rearrange("(p i) c -> p i c", i=PACK)
         for u in range(2):
@@ -288,12 +324,19 @@ def tile_list_hoof_trim_slots_kernel(
                     rhs=xq1[u][0][:].bitcast(FP8X4), rhs_scale=xq1[u][1][:], start=False, stop=True,
                 )
                 need = ring.tile([P, MH], F32, name=f"need{u}{i}", tag="need", bufs=4)
-                nc.scalar.activation(out=need[:], in_=y[:], func=ACT.Abs)
-                nc.scalar.activation(out=need[:], in_=need[:], func=ACT.Ln, bias=1.0)
+                size = need
+                if u == 0 and i == 0:
+                    size = ring.tile([P, MH], F32, name="size00", tag="handover", bufs=1, align_bytes=64)
+                nc.scalar.activation(out=size[:], in_=y[:], func=ACT.Abs)
+                nc.scalar.activation(out=need[:], in_=size[:], func=ACT.Ln, bias=1.0)
                 nc.scalar.activation(out=need[:], in_=need[:], func=ACT.Identity, bias=base_sb[:, i : i + 1])
                 nc.vector.tensor_tensor(
                     out=pages[i][:].indirect(idx3[:, u * MH // 16 : (u + 1) * MH // 16]),
                     in0=need[:], in1=wgo_sb[:, ms], op=ALU.mult,
                 )
+                if u == 0 and i == 0:
+                    st = ring.tile([P, PACK * MH], BF16, name="x_st11", tag="handover", bufs=1, align_bytes=64)
+                    interleave("scalar", st[:], picked11[:].rearrange("p (j c) -> p j c", j=PACK))
+                    xq1[1] = quantise(st[:], MH, "xq11")
                 if u == 1:
                     nc.sync.dma_start(out=out_rows[:, i, :], in_=pages[i][:])

@@ -42,7 +42,7 @@ def tile_list_hoof_trim_slots_kernel(
             return keep.tile(shape, dtype, name=name, align_bytes=64)
 
         def raw_tile(width, name):
-            return ring.tile([P, PACK, width], F32, name=name, tag="raw", bufs=5, align_bytes=64)
+            return ring.tile([P, PACK, width], F32, name=name, tag="raw", bufs=3, align_bytes=64)
 
         def stage_tile(width, name):
             return ring.tile([P, PACK * width], BF16, name=name, tag="stage", bufs=3, align_bytes=64)
@@ -61,8 +61,14 @@ def tile_list_hoof_trim_slots_kernel(
                     in_=scales[:, 4 * q : 4 * q + 4, :].bitcast(I32),
                 )
 
-        def load_rows(src, a, cols, name):
-            raw = raw_tile(HALF, name)
+        def room(i, shape, name):
+            return keep.tile(shape, F32, name=name, tag=f"room{i}", align_bytes=64)
+
+        def load_rows(src, a, cols, name, room_of=None):
+            if room_of is None:
+                raw = raw_tile(HALF, name)
+            else:
+                raw = room(room_of, [P, PACK, HALF], name)
             nc.sync.dma_start(
                 out=raw[:],
                 in_=src[a * PASS : (a + 1) * PASS, cols * HALF : (cols + 1) * HALF].rearrange("(p j) c -> p j c", j=PACK),
@@ -85,8 +91,8 @@ def tile_list_hoof_trim_slots_kernel(
         def deal(engine, st, raw):
             copy_on(
                 engine,
-                st.rearrange("p (t m j) -> p m j t", t=PACK, j=PACK),
-                raw[:].rearrange("p j (m t) -> p m j t", t=PACK),
+                st.rearrange("p (t m j) -> p m t j", t=PACK, j=PACK),
+                raw[:].rearrange("p j (m t) -> p m t j", t=PACK),
             )
 
         def round_plain(engine, raw, width, name):
@@ -118,18 +124,11 @@ def tile_list_hoof_trim_slots_kernel(
         w2_raw = {}
         sound_raw = {}
         tab = {}
-        def load_w1_words(b):
-            w1_raw[b] = kept([P, 2, 2 * HALF], U8, f"w1_raw{b}")
-            nc.sync.dma_start(
-                out=w1_raw[b][:].bitcast(I32),
-                in_=w1_words[:, :, 2 * HALF * b : 2 * HALF * (b + 1)].rearrange("a p c -> p a c").bitcast(I32),
-            )
-
-        w1_raw = {}
         nc.sync.dma_start(idx[:], offs)
         for a in range(2):
             w2_raw[0, a] = load_rows(w2, a, 0, f"w2_raw0{a}")
-        load_w1_words(0)
+        w1_raw = kept([P, 2, 2 * H], U8, "w1_raw")
+        nc.sync.dma_start(out=w1_raw[:].bitcast(I32), in_=w1_words.rearrange("a p c -> p a c").bitcast(I32))
         gain_sb = kept([P, 2, PACK], F32, "gain_sb")
         nc.sync.dma_start(out=gain_sb[:], in_=gain.rearrange("(b p i) -> p b i", b=2, i=PACK))
         wgt_sb = kept([P, M], F32, "wgt_sb")
@@ -145,11 +144,10 @@ def tile_list_hoof_trim_slots_kernel(
         load_packed_scale_rows(nc.sync, w3_sc_raw, w3_scales)
         for c in range(2):
             for a in range(2):
-                sound_raw[c, a] = load_rows(sound, a, c, f"sound_raw{c}{a}")
-        load_w1_words(1)
+                sound_raw[c, a] = load_rows(sound, a, c, f"sound_raw{c}{a}", 1 - a if c == 1 else None)
         for a in range(2):
-            w2_raw[1, a] = load_rows(w2, a, 1, f"w2_raw1{a}")
-        w3_raw = kept([P, 2, N], I32, "w3_raw")
+            w2_raw[1, a] = load_rows(w2, a, 1, f"w2_raw1{a}", 2 + a)
+        w3_raw = ring.tile([P, 2, N], I32, name="w3_raw", tag="raw", bufs=3, align_bytes=64)
         nc.sync.dma_start(out=w3_raw[:], in_=w3_words.rearrange("a p c i -> p a (c i)").bitcast(I32))
         base_sb = kept([P, PACK], F32, "base_sb")
         nc.sync.dma_start(out=base_sb[:], in_=base.rearrange("(p i) -> p i", i=PACK))
@@ -161,22 +159,16 @@ def tile_list_hoof_trim_slots_kernel(
         for a in range(2):
             w2q[0, a] = quantise(round_dealt("scalar", w2_raw[0, a], f"w2_st0{a}"), HALF, f"w2q0{a}")
 
-        w1c = {}
+        w1c = kept([P, 2, H], U16, "w1c")
         w1s = kept([P, 2, H], U8, "w1s")
-
-        def deal_w1_words(engine, b):
-            w1c[b] = kept([P, 2, HALF], U16, f"w1c{b}")
-            copy_on(
-                engine,
-                w1c[b][:].rearrange("p a (t m) -> p a t m", t=PACK),
-                w1_raw[b][:].bitcast(U16).rearrange("p a (m t) -> p a t m", t=PACK),
-            )
-
-        deal_w1_words("vector", 0)
+        nc.vector.tensor_copy(
+            out=w1c[:].rearrange("p a (b t m) -> p (a b) t m", b=2, t=PACK),
+            in_=w1_raw[:].bitcast(U16).rearrange("p a (b m t) -> p (a b) t m", b=2, t=PACK),
+        )
         for a in range(2):
             nc.vector.tensor_copy(out=v_sc[a][:], in_=tab_sc[:, a, :].indirect(idx[:]))
 
-        h = {(b, i): kept([P, S], F32, f"h{b}{i}") for b in range(2) for i in range(PACK)}
+        h = {(0, i): kept([P, S], F32, f"h0{i}") for i in range(PACK)}
         v_c = {}
 
         def product_given(b, i, c, tag):
@@ -197,7 +189,7 @@ def tile_list_hoof_trim_slots_kernel(
             for a in range(2):
                 nc.tensor.matmul_mx(
                     out=acc[:],
-                    lhsT=w1c[b][:, a, P * i : P * (i + 1)].bitcast(FP4X4), lhsT_scale=w1s[:, a, c0 : c0 + P],
+                    lhsT=w1c[:, a, c0 : c0 + P].bitcast(FP4X4), lhsT_scale=w1s[:, a, c0 : c0 + P],
                     rhs=v_c[c, a][:].bitcast(FP8X4), rhs_scale=v_sc[a][:, c * HALF : (c + 1) * HALF],
                     start=(a == 0), stop=(a == 1),
                 )
@@ -219,6 +211,7 @@ def tile_list_hoof_trim_slots_kernel(
             )
 
         picked11 = kept([P, PACK * MH], F32, "picked11")
+        x0_room = kept([P, 5 * MH], F32, "x0_room")
         wg = {}
         for b in range(2):
             for i in range(PACK):
@@ -229,9 +222,12 @@ def tile_list_hoof_trim_slots_kernel(
                     for u in range(2):
                         nc.scalar.activation(out=wg[b, i][u], in_=wgt_sb[:, u * MH : (u + 1) * MH], func=ACT.Copy, scale=scale)
                 else:
-                    both = kept([P, M], F32, f"wg{b}{i}")
-                    wg[b, i] = [both[:, 0:MH], both[:, MH:M], both[:]]
-                    nc.scalar.activation(out=both[:], in_=wgt_sb[:], func=ACT.Copy, scale=scale)
+                    if (b, i) == (1, 0):
+                        both = x0_room[:, 3 * MH : 5 * MH]
+                    else:
+                        both = kept([P, M], F32, f"wg{b}{i}")[:]
+                    wg[b, i] = [both[:, 0:MH], both[:, MH:M], both]
+                    nc.scalar.activation(out=both, in_=wgt_sb[:], func=ACT.Copy, scale=scale)
 
         for c in range(2):
             pick_words(0, c)
@@ -263,7 +259,6 @@ def tile_list_hoof_trim_slots_kernel(
             interleave(engine, st[:], sound_raw[1, 1][:, :, cols])
             nc.vector.quantize_mx(out=last_codes[:, cols].bitcast(FP8X4), scales=last_scales[:, cols], in_=st[:])
         soundq[1, 1] = (last_codes, last_scales)
-        deal_w1_words("scalar", 1)
 
         def pick_x(dst, b, i, first, count):
             nc.vector.tensor_tensor(
@@ -273,23 +268,22 @@ def tile_list_hoof_trim_slots_kernel(
                 op=ALU.mult,
             )
 
-        picked0 = kept([P, 5 * M], F32, "picked0")
+        picked0 = kept([P, PACK * M], F32, "picked0")
         for i in range(PACK):
             meet(product_given, 0, i, 1)
-            if i < PACK - 1:
+            if i < 2:
                 pick_x(picked0[:, i * M : (i + 1) * M], 0, i, 0, M)
         w2q[1, 0] = quantise(round_dealt("scalar", w2_raw[1, 0], "w2_st10"), HALF, "w2q10")
-        st = picked0[:, 3 * M : 5 * M].bitcast(BF16)
+        st = picked0[:, 2 * M : 4 * M].bitcast(BF16)
         deal("scalar", st, w2_raw[1, 1])
         w2q[1, 1] = quantise(st, HALF, "w2q11")
-        pick_x(picked0[:, 3 * M : 4 * M], 0, 3, 0, M)
+        for i in range(2, PACK):
+            pick_x(picked0[:, i * M : (i + 1) * M], 0, i, 0, M)
 
         for i in range(PACK):
+            h[1, i] = room(i, [P, S], f"h1{i}")
             for c in range(2):
                 park(product_picked, 1, i, c)
-        st = stage_tile(M, "x_st0")
-        interleave("scalar", st[:], picked0[:, 0 : PACK * M].rearrange("p (j c) -> p j c", j=PACK))
-        xq0 = quantise(st[:], M, "xq0")
         w3c = kept([P, 2, N], U32, "w3c")
         nc.scalar.copy(
             out=w3c[:].rearrange("p a (t m) -> p a t m", t=PACK),
@@ -301,6 +295,11 @@ def tile_list_hoof_trim_slots_kernel(
             for c in range(2):
                 meet(product_given, 1, i, c)
             pick_x(picked10[:, i, :], 1, i, 0, MH)
+            if i == 0:
+                st = x0_room[:, 0 : 4 * MH].bitcast(BF16)
+                interleave("scalar", st, picked0[:, 0 : PACK * M].rearrange("p (j c) -> p j c", j=PACK))
+            if i == 2:
+                xq0 = quantise(st, M, "xq0")
         for i in range(2):
             pick_x(picked11[:, i * MH : (i + 1) * MH], 1, i, MH, MH)
         st = picked11[:, 2 * MH : 4 * MH].bitcast(BF16)

@@ -121,6 +121,9 @@ def tile_list_hoof_trim_slots_kernel(
         for page in pages:
             nc.vector.memset(page[:], 0.0)
 
+        warm = kept([P, 2], F32, "warm")
+        nc.gpsimd.memset(warm[:, 0:1], 1.0)
+        nc.scalar.activation(out=warm[:, 1:2], in_=warm[:, 0:1], func=ACT.Ln)
         w2_raw = {}
         sound_raw = {}
         tab = {}

from contextlib import ExitStack

import concourse.mybir as mybir

K, H, N, T, S, M, T2 = 1024, 1024, 512, 4096, 1024, 512, 1024
FLOPS = 2 * (2 * K * H * S + H * N * M)

F32 = mybir.dt.float32
BF16 = mybir.dt.bfloat16
I32 = mybir.dt.int32
U32 = mybir.dt.uint32
U16 = mybir.dt.uint16
U8 = mybir.dt.uint8
FP8X4 = mybir.dt.float8_e4m3fn_x4
FP4X4 = mybir.dt.float4_e2m1fn_x4
ACT = mybir.ActivationFunctionType
ALU = mybir.AluOpType

P = 128
PACK = 4
PASS = P * PACK
HALF = 512
MH = M // 2


def tile_list_hoof_trim_slots_kernel(
    tc, tab_words, tab_scales, offs, w1_words, w1_scales, sound, w2, offs2, wgt, gain,
    w3_words, w3_scales, base, offs3, wgo, out,
):
    nc = tc.nc
    with ExitStack() as ctx:
        lists = ctx.enter_context(tc.tile_pool(name="lists", bufs=1))
        keep = ctx.enter_context(tc.tile_pool(name="keep", bufs=1))
        ring = ctx.enter_context(tc.tile_pool(name="ring", bufs=1))
        psum = ctx.enter_context(tc.psum_pool(name="psum", bufs=4))

        idx = lists.tile([P, S // 16], U16, name="idx")
        idx2 = lists.tile([P, M // 16], U16, name="idx2")
        idx3 = lists.tile([P, M // 16], U16, name="idx3")

        def kept(shape, dtype, name):
            return keep.tile(shape, dtype, name=name, align_bytes=64)

        def raw_tile(width, name):
            return ring.tile([P, PACK, width], F32, name=name, tag="raw", bufs=3, align_bytes=64)

        def stage_tile(width, name):
            return ring.tile([P, PACK * width], BF16, name=name, tag="stage", bufs=3, align_bytes=64)

        def load_scale_rows(queue, plane, scales):
            for q in range(4):
                queue.dma_start(
                    out=plane[32 * q : 32 * q + 4, :, :].bitcast(I32),
                    in_=scales[:, 4 * q : 4 * q + 4, :].rearrange("a r c -> r a c").bitcast(I32),
                )

        def load_packed_scale_rows(queue, plane, scales):
            for q in range(4):
                queue.dma_start(
                    out=plane[32 * q : 32 * q + 8, :].bitcast(I32),
                    in_=scales[:, 4 * q : 4 * q + 4, :].bitcast(I32),
                )

        def room(i, shape, name):
            return keep.tile(shape, F32, name=name, tag=f"room{i}", align_bytes=64)

        def load_rows(src, a, cols, name, room_of=None):
            if room_of is None:
                raw = raw_tile(HALF, name)
            else:
                raw = room(room_of, [P, PACK, HALF], name)
            nc.sync.dma_start(
                out=raw[:],
                in_=src[a * PASS : (a + 1) * PASS, cols * HALF : (cols + 1) * HALF].rearrange("(p j) c -> p j c", j=PACK),
            )
            return raw

        def copy_on(engine, out_ap, in_ap):
            if engine == "scalar":
                nc.scalar.copy(out=out_ap, in_=in_ap)
            else:
                nc.vector.tensor_copy(out=out_ap, in_=in_ap)

        def interleave(engine, st, rows):
            copy_on(
                engine,
                st.rearrange("p (c i j) -> p c j i", i=4, j=PACK),
                rows.rearrange("p j (c i) -> p c j i", i=4),
            )

        def deal(engine, st, raw):
            copy_on(
                engine,
                st.rearrange("p (t m j) -> p m t j", t=PACK, j=PACK),
                raw[:].rearrange("p j (m t) -> p m t j", t=PACK),
            )

        def round_plain(engine, raw, width, name):
            st = stage_tile(width, name)
            interleave(engine, st[:], raw[:])
            return st[:]

        def round_dealt(engine, raw, name):
            st = stage_tile(HALF, name)
            deal(engine, st[:], raw)
            return st[:]

        def quantise(st, width, name):
            codes = kept([P, width], U32, name + "_codes")
            scales = kept([P, width], U8, name + "_scales")
            nc.vector.quantize_mx(out=codes[:].bitcast(FP8X4), scales=scales[:], in_=st)
            return codes, scales

        tab_sc = kept([P, 2, T], U8, "tab_sc")
        w1_sc_raw = kept([P, 2, H], U8, "w1_sc_raw")
        w3_sc_raw = kept([P, N], U8, "w3_sc_raw")
        v_sc = {a: kept([P, S], U8, f"v_sc{a}") for a in range(2)}
        for plane in (tab_sc, w1_sc_raw, w3_sc_raw):
            nc.vector.memset(plane[:].bitcast(I32), 0)
        pages = [kept([P, T2], F32, f"page{i}") for i in range(PACK)]
        for page in pages:
            nc.vector.memset(page[:], 0.0)

        warm = kept([P, 2], F32, "warm")
        nc.gpsimd.memset(warm[:, 0:1], 1.0)
        nc.scalar.activation(out=warm[:, 1:2], in_=warm[:, 0:1], func=ACT.Ln)
        w2_raw = {}
        sound_raw = {}
        tab = {}
        nc.sync.dma_start(idx[:], offs)
        for a in range(2):
            w2_raw[0, a] = load_rows(w2, a, 0, f"w2_raw0{a}")
        w1_raw = kept([P, 2, 2 * H], U8, "w1_raw")
        nc.sync.dma_start(out=w1_raw[:].bitcast(I32), in_=w1_words.rearrange("a p c -> p a c").bitcast(I32))
        gain_sb = kept([P, 2, PACK], F32, "gain_sb")
        nc.sync.dma_start(out=gain_sb[:], in_=gain.rearrange("(b p i) -> p b i", b=2, i=PACK))
        wgt_sb = kept([P, M], F32, "wgt_sb")
        nc.sync.dma_start(out=wgt_sb[:], in_=wgt)
        nc.sync.dma_start(idx2[:], offs2)
        nc.sync.dma_start(idx3[:], offs3)
        load_scale_rows(nc.sync, tab_sc, tab_scales)
        for a in range(2):
            tab[a] = kept([P, T], I32, f"tab{a}")
            nc.sync.dma_start(out=tab[a][:], in_=tab_words[a].rearrange("p t i -> p (t i)").bitcast(I32))
            if a == 0:
                load_scale_rows(nc.sync, w1_sc_raw, w1_scales)
        load_packed_scale_rows(nc.sync, w3_sc_raw, w3_scales)
        for c in range(2):
            for a in range(2):
                sound_raw[c, a] = load_rows(sound, a, c, f"sound_raw{c}{a}", 1 - a if c == 1 else None)
        for a in range(2):
            w2_raw[1, a] = load_rows(w2, a, 1, f"w2_raw1{a}", 2 + a)
        w3_raw = ring.tile([P, 2, N], I32, name="w3_raw", tag="raw", bufs=3, align_bytes=64)
        nc.sync.dma_start(out=w3_raw[:], in_=w3_words.rearrange("a p c i -> p a (c i)").bitcast(I32))
        base_sb = kept([P, PACK], F32, "base_sb")
        nc.sync.dma_start(out=base_sb[:], in_=base.rearrange("(p i) -> p i", i=PACK))
        wgo_sb = kept([P, M], F32, "wgo_sb")
        nc.sync.dma_start(out=wgo_sb[:], in_=wgo)

        w2q = {}
        soundq = {}
        for a in range(2):
            w2q[0, a] = quantise(round_dealt("scalar", w2_raw[0, a], f"w2_st0{a}"), HALF, f"w2q0{a}")

        w1c = kept([P, 2, H], U16, "w1c")
        w1s = kept([P, 2, H], U8, "w1s")
        nc.vector.tensor_copy(
            out=w1c[:].rearrange("p a (b t m) -> p (a b) t m", b=2, t=PACK),
            in_=w1_raw[:].bitcast(U16).rearrange("p a (b m t) -> p (a b) t m", b=2, t=PACK),
        )
        for a in range(2):
            nc.vector.tensor_copy(out=v_sc[a][:], in_=tab_sc[:, a, :].indirect(idx[:]))

        h = {(0, i): kept([P, S], F32, f"h0{i}") for i in range(PACK)}
        v_c = {}

        def product_given(b, i, c, tag):
            acc = psum.tile([P, HALF], F32, name=f"given{b}{i}{c}", tag=tag)
            cols = slice(P * i, P * (i + 1))
            for a in range(2):
                nc.tensor.matmul_mx(
                    out=acc[:],
                    lhsT=w2q[b, a][0][:, cols].bitcast(FP8X4), lhsT_scale=w2q[b, a][1][:, cols],
                    rhs=soundq[c, a][0][:].bitcast(FP8X4), rhs_scale=soundq[c, a][1][:],
                    start=(a == 0), stop=(a == 1),
                )
            return acc

        def product_picked(b, i, c, tag):
            acc = psum.tile([P, HALF], F32, name=f"picked{b}{i}{c}", tag=tag)
            c0 = HALF * b + P * i
            for a in range(2):
                nc.tensor.matmul_mx(
                    out=acc[:],
                    lhsT=w1c[:, a, c0 : c0 + P].bitcast(FP4X4), lhsT_scale=w1s[:, a, c0 : c0 + P],
                    rhs=v_c[c, a][:].bitcast(FP8X4), rhs_scale=v_sc[a][:, c * HALF : (c + 1) * HALF],
                    start=(a == 0), stop=(a == 1),
                )
            return acc

        def h_cols(b, i, c):
            return h[b, i][:, c * HALF : (c + 1) * HALF]

        def park(product, b, i, c):
            nc.scalar.copy(out=h_cols(b, i, c), in_=product(b, i, c, "early")[:])

        def meet(product, b, i, c):
            nc.vector.tensor_tensor(out=h_cols(b, i, c), in0=product(b, i, c, "late")[:], in1=h_cols(b, i, c), op=ALU.max)

        def pick_words(a, c):
            v_c[c, a] = kept([P, HALF], U32, f"v_c{c}{a}")
            nc.vector.tensor_copy(
                out=v_c[c, a][:], in_=tab[a][:].bitcast(U32).indirect(idx[:, c * HALF // 16 : (c + 1) * HALF // 16])
            )

        picked11 = kept([P, PACK * MH], F32, "picked11")
        x0_room = kept([P, 5 * MH], F32, "x0_room")
        wg = {}
        for b in range(2):
            for i in range(PACK):
                scale = gain_sb[:, b, i : i + 1]
                if (b, i) == (1, PACK - 1):
                    wg_last = kept([P, MH], F32, "wg_last")
                    wg[b, i] = [picked11[:, 0:MH], wg_last[:]]
                    for u in range(2):
                        nc.scalar.activation(out=wg[b, i][u], in_=wgt_sb[:, u * MH : (u + 1) * MH], func=ACT.Copy, scale=scale)
                else:
                    if (b, i) == (1, 0):
                        both = x0_room[:, 3 * MH : 5 * MH]
                    else:
                        both = kept([P, M], F32, f"wg{b}{i}")[:]
                    wg[b, i] = [both[:, 0:MH], both[:, MH:M], both]
                    nc.scalar.activation(out=both, in_=wgt_sb[:], func=ACT.Copy, scale=scale)

        for c in range(2):
            pick_words(0, c)
        nc.vector.tensor_copy(
            out=w1s[:].rearrange("p a (b t m) -> p (a b) t m", b=2, t=PACK),
            in_=w1_sc_raw[:].rearrange("p a (b m t) -> p (a b) t m", b=2, t=PACK),
        )
        for c in range(2):
            pick_words(1, c)
        w3s = kept([P, N], U8, "w3s")
        nc.vector.tensor_copy(
            out=w3s[:].rearrange("p (t m) -> p t m", t=PACK),
            in_=w3_sc_raw[:].rearrange("p (m t) -> p t m", t=PACK),
        )
        for c in range(2):
            for i in range(PACK):
                park(product_picked, 0, i, c)

        for a in range(2):
            soundq[0, a] = quantise(round_plain("vector", sound_raw[0, a], HALF, f"sound_st0{a}"), HALF, f"soundq0{a}")
        for i in range(PACK):
            meet(product_given, 0, i, 0)
        soundq[1, 0] = quantise(round_plain("scalar", sound_raw[1, 0], HALF, "sound_st10"), HALF, "soundq10")
        last_codes = kept([P, HALF], U32, "soundq11_codes")
        last_scales = kept([P, HALF], U8, "soundq11_scales")
        for part, engine in enumerate(("vector", "scalar")):
            cols = slice(part * MH, (part + 1) * MH)
            st = stage_tile(MH, f"sound_st11{part}")
            interleave(engine, st[:], sound_raw[1, 1][:, :, cols])
            nc.vector.quantize_mx(out=last_codes[:, cols].bitcast(FP8X4), scales=last_scales[:, cols], in_=st[:])
        soundq[1, 1] = (last_codes, last_scales)

        def pick_x(dst, b, i, first, count):
            nc.vector.tensor_tensor(
                out=dst,
                in0=h[b, i][:].indirect(idx2[:, first // 16 : (first + count) // 16]),
                in1=wg[b, i][first // MH if count == MH else 2],
                op=ALU.mult,
            )

        picked0 = kept([P, PACK * M], F32, "picked0")
        for i in range(PACK):
            meet(product_given, 0, i, 1)
            if i < 2:
                pick_x(picked0[:, i * M : (i + 1) * M], 0, i, 0, M)
        w2q[1, 0] = quantise(round_dealt("scalar", w2_raw[1, 0], "w2_st10"), HALF, "w2q10")
        st = picked0[:, 2 * M : 4 * M].bitcast(BF16)
        deal("scalar", st, w2_raw[1, 1])
        w2q[1, 1] = quantise(st, HALF, "w2q11")
        for i in range(2, PACK):
            pick_x(picked0[:, i * M : (i + 1) * M], 0, i, 0, M)

        for i in range(PACK):
            h[1, i] = room(i, [P, S], f"h1{i}")
            for c in range(2):
                park(product_picked, 1, i, c)
        w3c = kept([P, 2, N], U32, "w3c")
        nc.scalar.copy(
            out=w3c[:].rearrange("p a (t m) -> p a t m", t=PACK),
            in_=w3_raw[:].bitcast(U32).rearrange("p a (m t) -> p a t m", t=PACK),
        )

        picked10 = raw_tile(MH, "picked10")
        for i in range(PACK):
            for c in range(2):
                meet(product_given, 1, i, c)
            pick_x(picked10[:, i, :], 1, i, 0, MH)
            if i == 0:
                st = x0_room[:, 0 : 4 * MH].bitcast(BF16)
                interleave("scalar", st, picked0[:, 0 : PACK * M].rearrange("p (j c) -> p j c", j=PACK))
            if i == 2:
                xq0 = quantise(st, M, "xq0")
        for i in range(2):
            pick_x(picked11[:, i * MH : (i + 1) * MH], 1, i, MH, MH)
        st = picked11[:, 2 * MH : 4 * MH].bitcast(BF16)
        interleave("scalar", st, picked10[:])
        xq1 = {0: quantise(st, MH, "xq10")}
        for i in range(2, PACK):
            pick_x(picked11[:, i * MH : (i + 1) * MH], 1, i, MH, MH)

        out_rows = out.rearrange("(p i) c -> p i c", i=PACK)
        for u in range(2):
            ms = slice(u * MH, (u + 1) * MH)
            for i in range(PACK):
                cols = slice(P * i, P * (i + 1))
                y = psum.tile([P, MH], F32, name=f"y{u}{i}", tag="early")
                nc.tensor.matmul_mx(
                    out=y[:], lhsT=w3c[:, 0, cols].bitcast(FP8X4), lhsT_scale=w3s[:, cols],
                    rhs=xq0[0][:, ms].bitcast(FP8X4), rhs_scale=xq0[1][:, ms], start=True, stop=False,
                )
                nc.tensor.matmul_mx(
                    out=y[:], lhsT=w3c[:, 1, cols].bitcast(FP8X4), lhsT_scale=w3s[4:P, cols],
                    rhs=xq1[u][0][:].bitcast(FP8X4), rhs_scale=xq1[u][1][:], start=False, stop=True,
                )
                need = ring.tile([P, MH], F32, name=f"need{u}{i}", tag="need", bufs=4)
                size = need
                if u == 0 and i == 0:
                    size = ring.tile([P, MH], F32, name="size00", tag="handover", bufs=1, align_bytes=64)
                nc.scalar.activation(out=size[:], in_=y[:], func=ACT.Abs)
                nc.scalar.activation(out=need[:], in_=size[:], func=ACT.Ln, bias=1.0)
                nc.scalar.activation(out=need[:], in_=need[:], func=ACT.Identity, bias=base_sb[:, i : i + 1])
                nc.vector.tensor_tensor(
                    out=pages[i][:].indirect(idx3[:, u * MH // 16 : (u + 1) * MH // 16]),
                    in0=need[:], in1=wgo_sb[:, ms], op=ALU.mult,
                )
                if u == 0 and i == 0:
                    st = ring.tile([P, PACK * MH], BF16, name="x_st11", tag="handover", bufs=1, align_bytes=64)
                    interleave("scalar", st[:], picked11[:].rearrange("p (j c) -> p j c", j=PACK))
                    xq1[1] = quantise(st[:], MH, "xq11")
                if u == 1:
                    nc.sync.dma_start(out=out_rows[:, i, :], in_=pages[i][:])
